import numpy as np
import ml_dtypes


def mxq(x, axis, fmt="e4m3"):
    dtype, down = {"e4m3": (ml_dtypes.float8_e4m3fn, 7), "e5m2": (ml_dtypes.float8_e5m2, 14)}[fmt]
    v = np.moveaxis(np.asarray(x, np.float32).astype(ml_dtypes.bfloat16).astype(np.float64), axis, -1)
    blocks = v.reshape(v.shape[:-1] + (-1, 32))
    amax = np.abs(blocks).max(-1, keepdims=True)
    byte = np.maximum(np.where(amax > 0, np.frexp(amax)[1] - 1 + 127, 0) - down, 1)
    scale = np.exp2(byte - 127.0)
    codes = (blocks / scale).astype(np.float32).astype(dtype).astype(np.float64)
    return np.moveaxis((codes * scale).reshape(v.shape), -1, axis)


WIDE = False


def mx_kscale(k):
    if not WIDE:
        return np.ones(k)
    levels = np.array([10, -10, 5, -5, 0])
    if k % 512:
        return np.exp2(np.random.permutation(np.resize(levels, k // 32))).repeat(32)
    a = np.empty((k // 512, 16))
    for p in range(k // 512):
        a[p, :8] = np.random.permutation(np.resize(levels, 8))
        for g in range(8):
            far = levels[np.abs(levels - a[p, g]) >= 10]
            a[p, g + 8] = far[np.random.randint(len(far))]
    return np.exp2(a.ravel()).repeat(32)


def f64(x):
    return np.asarray(x).astype(np.float64)


def striped(idx):
    return np.tile(idx.reshape(-1, 16).T, (8, 1)).astype(np.uint16)


def unstriped(offs):
    return offs[:16].T.reshape(-1).astype(np.int64)


def pack_weight(w):
    k, n = w.shape
    w = f64(np.asarray(w, np.float32).astype(ml_dtypes.bfloat16)).reshape(k // 32, 32, n)
    amax = np.abs(w).max(1)
    byte = np.clip(np.where(amax > 0, np.frexp(amax)[1] - 1 + 127 - 7, 1), 1, 254)
    scaled = (w * np.exp2(127.0 - byte)[:, None, :]).reshape(k, n).astype(np.float32)
    words = np.ascontiguousarray(scaled.reshape(k // 512, 128, 4, n).transpose(0, 1, 3, 2)).astype(ml_dtypes.float8_e4m3fn).view(np.uint8)
    return words, np.ascontiguousarray(byte.astype(np.uint8).reshape(k // 512, 16, n))


def unpack_weight(words, scales):
    g, p, n, _ = words.shape
    vals = np.ascontiguousarray(words).view(ml_dtypes.float8_e4m3fn).astype(np.float64) * np.repeat(np.exp2(scales.astype(np.float64) - 127.0), 8, axis=1)[..., None]
    return vals.transpose(0, 1, 3, 2).reshape(g * 512, n)


def relu(v):
    return np.maximum(v, 0.0)


K, T, S, N, H = 1024, 2048, 512, 128, 512


def setup_inputs():
    n = np.random.standard_normal
    s = mx_kscale(K)[:, None]
    u = mx_kscale(H)
    packed_xT = pack_weight(n((K, T)) * s)
    return {
        "x_words": packed_xT[0],
        "x_scales": packed_xT[1],
        "w1": (n((K, H)) / np.sqrt(K) / s).astype(np.float32),
        "w2": (n((K, H)) / np.sqrt(K) / s).astype(np.float32),
        "minv": (np.random.uniform(0.3, 0.9, (H, S))).astype(np.float32),
        "lam0": (np.random.uniform(0.0, 1.0, (H, S))).astype(np.float32),
        "unit": (np.random.uniform(0.6, 1.4, (H, 1)) * u[:, None]).astype(np.float32),
        "w3": (n((H, N)) / np.sqrt(H) / u[:, None]).astype(np.float32),
        "offs": striped(np.random.permutation(T)[:S]),
        "bod": striped(np.random.permutation(S)),
    }


def reference(x_words, x_scales, w1, w2, minv, lam0, unit, w3, offs, bod):
    xq = unpack_weight(x_words, x_scales)[:, unstriped(offs)]
    vn = mxq(f64(w1), 0, "e4m3").T @ xq
    lam1 = relu(f64(lam0) - (f64(minv) * vn))
    lo = lam1[:, unstriped(bod)]
    dv = lo * (0.6 * f64(minv))
    lam2 = relu(lam1 - (f64(minv) * (vn + dv)))
    vt = mxq(f64(w2), 0, "e4m3").T @ xq
    cone = 0.6 * lam2
    fric = np.maximum(np.minimum(-1.0 * (f64(minv) * vt), cone), -1.0 * cone)
    hid = f64(unit) * (lam2 + fric)
    return mxq(f64(w3), 0, "e4m3").T @ mxq(hid, 0, "e4m3")

@@ -1,0 +1,201 @@
+from contextlib import ExitStack
+
+import concourse.mybir as mybir
+from concourse.masks import make_identity
+
+K, T, S, N, H = 1024, 2048, 512, 128, 512
+FLOPS = 2 * (2 * K * H * S + H * N * S)
+
+F32 = mybir.dt.float32
+BF16 = mybir.dt.bfloat16
+I32 = mybir.dt.int32
+U32 = mybir.dt.uint32
+U16 = mybir.dt.uint16
+U8 = mybir.dt.uint8
+FP8X4 = mybir.dt.float8_e4m3fn_x4
+ALU = mybir.AluOpType
+ACT = mybir.ActivationFunctionType
+
+P = 128
+PACK = 4
+PASSES = K // (P * PACK)
+HALF = S // 2
+
+
+def tile_picked_ycontc_sum_p_kernel(tc, x_words, x_scales, w1, w2, minv, lam0, unit, w3, offs, bod, out):
+    nc = tc.nc
+    with ExitStack() as ctx:
+        keep = ctx.enter_context(tc.tile_pool(name="keep", bufs=1))
+        work = ctx.enter_context(tc.tile_pool(name="work", bufs=4))
+        psum = ctx.enter_context(tc.psum_pool(name="psum", bufs=2))
+
+        def load_weight(w, name, o, parts):
+            raw = keep.tile([P, PACK, H], F32, name="%s_raw%d" % (name, o))
+            rows = w[512 * o : 512 * (o + 1), :].rearrange("(p j) c -> p j c", j=PACK)
+            step = PACK // parts
+            for j in range(0, PACK, step):
+                nc.sync.dma_start(out=raw[:, j : j + step, :], in_=rows[:, j : j + step, :])
+            return raw
+
+        def load_rows(src, name, t):
+            rows = keep.tile([P, S], F32, name="%s%d" % (name, t))
+            nc.sync.dma_start(out=rows[:], in_=src.rearrange("(p t) s -> p t s", t=PACK)[:, t, :])
+            return rows
+
+        def load_words(o):
+            tab = keep.tile([P, T], I32, name="word_tab%d" % o, align_bytes=64)
+            nc.sync.dma_start(out=tab[:], in_=x_words[o].rearrange("p n r -> p (n r)").bitcast(I32))
+            return tab
+
+        scale_tab = keep.tile([P, T], U8, name="scale_tab", align_bytes=64)
+        nc.vector.memset(scale_tab[:].bitcast(I32), 0)
+        ident = keep.tile([P, P], F32, name="ident")
+        make_identity(nc, ident[:])
+
+        offs_sb = keep.tile([P, S // 16], U16, name="offs_sb")
+        nc.sync.dma_start(offs_sb[:], offs)
+        unit_sb = keep.tile([P, PACK], F32, name="unit_sb")
+        nc.sync.dma_start(out=unit_sb[:], in_=unit.rearrange("(p t) o -> p (t o)", t=PACK))
+        bod_sb = keep.tile([P, S // 16], U16, name="bod_sb")
+        nc.sync.dma_start(bod_sb[:], bod)
+        w1_raw = [load_weight(w1, "w1", 0, 2)]
+        for q in range(4):
+            nc.sync.dma_start(out=scale_tab[32 * q : 32 * q + 4 * PASSES, :].bitcast(I32), in_=x_scales[:, 4 * q : 4 * q + 4, :].bitcast(I32))
+        w1_raw.append(load_weight(w1, "w1", 1, 2))
+        word_tab = [load_words(o) for o in range(PASSES)]
+        m_sb, l_sb, lam2, nb = {}, {}, {}, {}
+        m_sb[0] = load_rows(minv, "minv", 0)
+        l_sb[0] = load_rows(lam0, "lam0", 0)
+        m_sb[1] = load_rows(minv, "minv", 1)
+        l_sb[1] = load_rows(lam0, "lam0", 1)
+        w2_raw = [load_weight(w2, "w2", 0, 1)]
+        w2_raw.append(load_weight(w2, "w2", 1, 1))
+        m_sb[2] = load_rows(minv, "minv", 2)
+        l_sb[2] = load_rows(lam0, "lam0", 2)
+        m_sb[3] = load_rows(minv, "minv", 3)
+        l_sb[3] = load_rows(lam0, "lam0", 3)
+        w3_raw = keep.tile([P, PACK, N], F32, name="w3_raw")
+        nc.sync.dma_start(out=w3_raw[:], in_=w3.rearrange("(p j) c -> p j c", j=PACK))
+
+        def quantize(name, grouped, width):
+            codes = keep.tile([P, width], U32, name=name + "_codes", align_bytes=64)
+            scales = keep.tile([P, width], U8, name=name + "_scales", align_bytes=64)
+            nc.vector.quantize_mx(out=codes[:].bitcast(FP8X4), scales=scales[:], in_=grouped)
+            return codes, scales
+
+        def deal(name, raw, copy):
+            grouped = keep.tile([P, PACK * H], BF16, name=name + "_bf", align_bytes=64)
+            copy(out=grouped[:].rearrange("p (t m j) -> p m t j", t=PACK, j=PACK), in_=raw[:].rearrange("p j (m t) -> p m t j", t=PACK))
+            return grouped
+
+        w1_q = [quantize("w1q0", deal("w1g0", w1_raw[0], nc.scalar.copy)[:], H)]
+        x_scale = keep.tile([P, S], U8, name="x_scale", align_bytes=64)
+        nc.vector.tensor_copy(x_scale[:], scale_tab[:].indirect(offs_sb[:]))
+        x_code = []
+        for o in range(PASSES):
+            code = keep.tile([P, S], U32, name="x_code%d" % o, align_bytes=64)
+            nc.vector.tensor_copy(code[:], word_tab[o][:].bitcast(U32).indirect(offs_sb[:]))
+            x_code.append(code)
+        w1_q.append(quantize("w1q1", deal("w1g1", w1_raw[1], nc.vector.tensor_copy)[:], H))
+
+        def velocity(wq, t):
+            acc = psum.tile([P, S], F32, name="acc", tag="mm", bufs=3)
+            for o in range(PASSES):
+                codes, scales = wq[o]
+                nc.tensor.matmul_mx(
+                    out=acc[:],
+                    lhsT=codes[:, P * t : P * (t + 1)].bitcast(FP8X4),
+                    lhsT_scale=scales[:, P * t : P * (t + 1)],
+                    rhs=x_code[o][:].bitcast(FP8X4),
+                    rhs_scale=x_scale[4 * o : P, :],
+                    start=(o == 0),
+                    stop=(o == PASSES - 1),
+                )
+            return acc
+
+        cone_hi = keep.tile([P, PACK], F32, name="cone_hi")
+        cone_lo = keep.tile([P, PACK], F32, name="cone_lo")
+        neg_unit = keep.tile([P, PACK], F32, name="neg_unit")
+        nc.scalar.activation(cone_hi[:], unit_sb[:], ACT.Abs, scale=0.6)
+        nc.scalar.activation(cone_lo[:], cone_hi[:], ACT.Copy, scale=-1.0)
+        nc.scalar.activation(neg_unit[:], unit_sb[:], ACT.Copy, scale=-1.0)
+
+        def pieces(n):
+            return [slice(S // n * h, S // n * (h + 1)) for h in range(n)]
+
+        def sweeps(t, after, before):
+            vn = velocity(w1_q, t)
+            na = work.tile([P, S], F32, name="na")
+            nc.vector.scalar_tensor_tensor(na[:], vn[:], -1.0, m_sb[t][:], ALU.mult, ALU.mult)
+            m2 = work.tile([P, S], F32, name="m2")
+            nc.scalar.activation(m2[:], m_sb[t][:], ACT.Square)
+            d = work.tile([P, S], F32, name="d")
+            lam1 = work.tile([P, S], F32, name="lam1")
+            for cols in pieces(before):
+                nc.vector.tensor_tensor(d[:, cols], l_sb[t][:, cols], na[:, cols], ALU.add)
+                nc.scalar.activation(lam1[:, cols], d[:, cols], ACT.Relu)
+            lo = work.tile([P, S], F32, name="lo")
+            for h in range(2):
+                nc.scalar.activation(lo[:, HALF * h : HALF * (h + 1)], lam1[:].indirect(bod_sb[:, 16 * h : 16 * (h + 1)]), ACT.Copy)
+            ng = work.tile([P, S], F32, name="ng")
+            lam2_t = work.tile([P, S], F32, name="lam2_t")
+            banks = []
+            for cols in pieces(after):
+                width = cols.stop - cols.start
+                nc.vector.scalar_tensor_tensor(ng[:, cols], lo[:, cols], -0.6, m2[:, cols], ALU.mult, ALU.mult)
+                f_t = psum.tile([P, width], F32, name="f_t", bufs=2)
+                blocks = list(range(0, width, P))
+                for a, term in enumerate((na, lam1, ng)):
+                    for b in blocks:
+                        nc.tensor.matmul(f_t[:, b : b + P], term[:, cols.start + b : cols.start + b + P], ident[:], start=(a == 0 and b == 0), stop=(a == 2 and b == blocks[-1]), is_transpose=True)
+                nc.scalar.activation(lam2_t[:, cols], f_t[:], ACT.Relu)
+                bank = psum.tile([P, width], F32, name="lam2", bufs=3)
+                for b in blocks:
+                    nc.tensor.transpose(bank[:, b : b + P], lam2_t[:, cols.start + b : cols.start + b + P], ident[:])
+                banks.append((cols, bank))
+            return banks
+
+        hid_rows = keep.tile([P, PACK, S], BF16, name="hid_rows")
+
+        def tangent(t):
+            vt = velocity(w2_q, t)
+            nb_t = work.tile([P, S], F32, name="nb_t")
+            nc.vector.scalar_tensor_tensor(nb_t[:], vt[:], neg_unit[:, t : t + 1], m_sb[t][:], ALU.mult, ALU.mult)
+            return nb_t
+
+        def friction(t, banks, nb_t):
+            t1 = work.tile([P, S], F32, name="t1")
+            t2 = work.tile([P, S], F32, name="t2")
+            for cols, bank in banks:
+                nc.vector.scalar_tensor_tensor(t1[:, cols], bank[:], cone_hi[:, t : t + 1], nb_t[:, cols], ALU.mult, ALU.min)
+                nc.vector.scalar_tensor_tensor(t2[:, cols], bank[:], cone_lo[:, t : t + 1], t1[:, cols], ALU.mult, ALU.max)
+                nc.vector.scalar_tensor_tensor(hid_rows[:, t, cols], bank[:], unit_sb[:, t : t + 1], t2[:, cols], ALU.mult, ALU.add)
+
+        w2_q = [quantize("w2q0", deal("w2g0", w2_raw[0], nc.vector.tensor_copy)[:], H)]
+        w2_q.append(quantize("w2q1", deal("w2g1", w2_raw[1], nc.vector.tensor_copy)[:], H))
+        lam2[0] = sweeps(0, 1, 1)
+        lam2[1] = sweeps(1, 1, 1)
+        lam2[2] = sweeps(2, 1, 1)
+        lam2[3] = sweeps(3, 2, 2)
+        nb[0] = tangent(0)
+        friction(0, lam2[0], nb[0])
+        nb[1] = tangent(1)
+        friction(1, lam2[1], nb[1])
+        nb[2] = tangent(2)
+        friction(2, lam2[2], nb[2])
+        nb[3] = tangent(3)
+        w3_bf = keep.tile([P, N * PACK], BF16, name="w3_bf", align_bytes=64)
+        nc.scalar.copy(out=w3_bf[:].rearrange("p (c i j) -> p c j i", i=4, j=PACK), in_=w3_raw[:].rearrange("p j (c i) -> p c j i", i=4))
+        w3_codes, w3_scales = quantize("w3q", w3_bf[:], N)
+        friction(3, lam2[3], nb[3])
+
+        for h, copy in enumerate((nc.scalar.copy, nc.vector.tensor_copy)):
+            cols = slice(HALF * h, HALF * (h + 1))
+            hid = work.tile([P, HALF * PACK], BF16, name="hid", align_bytes=64)
+            copy(out=hid[:].rearrange("p (c i t) -> p c t i", i=4, t=PACK), in_=hid_rows[:, :, cols].rearrange("p t (c i) -> p c t i", i=4))
+            codes, scales = quantize("hid%d" % h, hid[:], HALF)
+            acc = psum.tile([P, HALF], F32, name="acc_out", tag="mm", bufs=3)
+            nc.tensor.matmul_mx(out=acc[:], lhsT=w3_codes[:].bitcast(FP8X4), lhsT_scale=w3_scales[:], rhs=codes[:].bitcast(FP8X4), rhs_scale=scales[:], start=True, stop=True)
+            res = work.tile([P, HALF], F32, name="res")
+            nc.scalar.copy(out=res[:], in_=acc[:])
+            nc.sync.dma_start(out=out[:, cols], in_=res[:])

@@ -27,19 +27,23 @@ def tile_picked_ycontc_sum_p_kernel(tc, x_words, x_scales, w1, w2, minv, lam0, u
     with ExitStack() as ctx:
         keep = ctx.enter_context(tc.tile_pool(name="keep", bufs=1))
         work = ctx.enter_context(tc.tile_pool(name="work", bufs=4))
-        psum = ctx.enter_context(tc.psum_pool(name="psum", bufs=2))
+        psum = ctx.enter_context(tc.psum_pool(name="psum", bufs=1))
+        banks = {"mm": 3, "ft": 3, "nbk": 2, "bk": 1}
 
-        def load_weight(w, name, o, parts):
-            raw = keep.tile([P, PACK, H], F32, name="%s_raw%d" % (name, o))
-            rows = w[512 * o : 512 * (o + 1), :].rearrange("(p j) c -> p j c", j=PACK)
-            step = PACK // parts
-            for j in range(0, PACK, step):
-                nc.sync.dma_start(out=raw[:, j : j + step, :], in_=rows[:, j : j + step, :])
-            return raw
+        def bank(tag, width):
+            return psum.tile([P, width], F32, name="bank_" + tag, tag=tag, bufs=banks[tag])
 
-        def load_rows(src, name, t):
-            rows = keep.tile([P, S], F32, name="%s%d" % (name, t))
-            nc.sync.dma_start(out=rows[:], in_=src.rearrange("(p t) s -> p t s", t=PACK)[:, t, :])
+        def load_weight(w, name, h):
+            tiles = []
+            for o in range(PASSES):
+                tile = keep.tile([P, PACK, H // 2], F32, name="%s_raw%d%d" % (name, h, o))
+                nc.sync.dma_start(out=tile[:], in_=w[512 * o : 512 * (o + 1), H // 2 * h : H // 2 * (h + 1)].rearrange("(p j) c -> p j c", j=PACK))
+                tiles.append(tile)
+            return tiles
+
+        def load_rows(src, name, c):
+            rows = keep.tile([P, S], F32, name="%s%d" % (name, c))
+            nc.sync.dma_start(out=rows[:], in_=src[P * c : P * (c + 1), :])
             return rows
 
         def load_words(o):
@@ -48,47 +52,51 @@ def tile_picked_ycontc_sum_p_kernel(tc, x_words, x_scales, w1, w2, minv, lam0, u
             return tab
 
         scale_tab = keep.tile([P, T], U8, name="scale_tab", align_bytes=64)
-        nc.vector.memset(scale_tab[:].bitcast(I32), 0)
+        nc.gpsimd.memset(scale_tab[:].bitcast(I32), 0)
         ident = keep.tile([P, P], F32, name="ident")
         make_identity(nc, ident[:])
 
+        raw, wq, m_sb, l_sb, nb_t = {}, {}, {}, {}, {}
         offs_sb = keep.tile([P, S // 16], U16, name="offs_sb")
         nc.sync.dma_start(offs_sb[:], offs)
         unit_sb = keep.tile([P, PACK], F32, name="unit_sb")
         nc.sync.dma_start(out=unit_sb[:], in_=unit.rearrange("(p t) o -> p (t o)", t=PACK))
         bod_sb = keep.tile([P, S // 16], U16, name="bod_sb")
         nc.sync.dma_start(bod_sb[:], bod)
-        w1_raw = [load_weight(w1, "w1", 0, 2)]
+        raw["w1", 0] = load_weight(w1, "w1", 0)
         for q in range(4):
             nc.sync.dma_start(out=scale_tab[32 * q : 32 * q + 4 * PASSES, :].bitcast(I32), in_=x_scales[:, 4 * q : 4 * q + 4, :].bitcast(I32))
-        w1_raw.append(load_weight(w1, "w1", 1, 2))
         word_tab = [load_words(o) for o in range(PASSES)]
-        m_sb, l_sb, lam2, nb = {}, {}, {}, {}
         m_sb[0] = load_rows(minv, "minv", 0)
         l_sb[0] = load_rows(lam0, "lam0", 0)
+        raw["w2", 0] = load_weight(w2, "w2", 0)
         m_sb[1] = load_rows(minv, "minv", 1)
         l_sb[1] = load_rows(lam0, "lam0", 1)
-        w2_raw = [load_weight(w2, "w2", 0, 1)]
-        w2_raw.append(load_weight(w2, "w2", 1, 1))
+        raw["w1", 1] = load_weight(w1, "w1", 1)
         m_sb[2] = load_rows(minv, "minv", 2)
         l_sb[2] = load_rows(lam0, "lam0", 2)
+        raw["w2", 1] = load_weight(w2, "w2", 1)
         m_sb[3] = load_rows(minv, "minv", 3)
         l_sb[3] = load_rows(lam0, "lam0", 3)
         w3_raw = keep.tile([P, PACK, N], F32, name="w3_raw")
         nc.sync.dma_start(out=w3_raw[:], in_=w3.rearrange("(p j) c -> p j c", j=PACK))
 
-        def quantize(name, grouped, width):
+        def quantize(name, grouped):
+            width = grouped.shape[1] // PACK
             codes = keep.tile([P, width], U32, name=name + "_codes", align_bytes=64)
             scales = keep.tile([P, width], U8, name=name + "_scales", align_bytes=64)
-            nc.vector.quantize_mx(out=codes[:].bitcast(FP8X4), scales=scales[:], in_=grouped)
+            nc.vector.quantize_mx(out=codes[:].bitcast(FP8X4), scales=scales[:], in_=grouped[:])
             return codes, scales
 
-        def deal(name, raw, copy):
-            grouped = keep.tile([P, PACK * H], BF16, name=name + "_bf", align_bytes=64)
-            copy(out=grouped[:].rearrange("p (t m j) -> p m t j", t=PACK, j=PACK), in_=raw[:].rearrange("p j (m t) -> p m t j", t=PACK))
+        def interleave(name, rows, copy):
+            grouped = keep.tile([P, PACK * rows.shape[2]], BF16, name=name + "_bf", align_bytes=64)
+            copy(out=grouped[:].rearrange("p (c i j) -> p c j i", i=4, j=PACK), in_=rows[:].rearrange("p j (c i) -> p c j i", i=4))
             return grouped
 
-        w1_q = [quantize("w1q0", deal("w1g0", w1_raw[0], nc.scalar.copy)[:], H)]
+        def weight_codes(name, h, copies):
+            return [quantize("%s_%d%d" % (name, h, o), interleave("%s_%d%d" % (name, h, o), raw[name, h][o], copies[o])) for o in range(PASSES)]
+
+        wq["w1", 0] = weight_codes("w1", 0, (nc.scalar.copy, nc.scalar.copy))
         x_scale = keep.tile([P, S], U8, name="x_scale", align_bytes=64)
         nc.vector.tensor_copy(x_scale[:], scale_tab[:].indirect(offs_sb[:]))
         x_code = []
@@ -96,16 +104,16 @@ def tile_picked_ycontc_sum_p_kernel(tc, x_words, x_scales, w1, w2, minv, lam0, u
             code = keep.tile([P, S], U32, name="x_code%d" % o, align_bytes=64)
             nc.vector.tensor_copy(code[:], word_tab[o][:].bitcast(U32).indirect(offs_sb[:]))
             x_code.append(code)
-        w1_q.append(quantize("w1q1", deal("w1g1", w1_raw[1], nc.vector.tensor_copy)[:], H))
 
-        def velocity(wq, t):
-            acc = psum.tile([P, S], F32, name="acc", tag="mm", bufs=3)
+        def velocity(name, c):
+            acc = bank("mm", S)
+            cols = slice(P * (c % 2), P * (c % 2 + 1))
             for o in range(PASSES):
-                codes, scales = wq[o]
+                codes, scales = wq[name, c // 2][o]
                 nc.tensor.matmul_mx(
                     out=acc[:],
-                    lhsT=codes[:, P * t : P * (t + 1)].bitcast(FP8X4),
-                    lhsT_scale=scales[:, P * t : P * (t + 1)],
+                    lhsT=codes[:, cols].bitcast(FP8X4),
+                    lhsT_scale=scales[:, cols],
                     rhs=x_code[o][:].bitcast(FP8X4),
                     rhs_scale=x_scale[4 * o : P, :],
                     start=(o == 0),
@@ -113,89 +121,92 @@ def tile_picked_ycontc_sum_p_kernel(tc, x_words, x_scales, w1, w2, minv, lam0, u
                 )
             return acc
 
-        cone_hi = keep.tile([P, PACK], F32, name="cone_hi")
-        cone_lo = keep.tile([P, PACK], F32, name="cone_lo")
-        neg_unit = keep.tile([P, PACK], F32, name="neg_unit")
-        nc.scalar.activation(cone_hi[:], unit_sb[:], ACT.Abs, scale=0.6)
-        nc.scalar.activation(cone_lo[:], cone_hi[:], ACT.Copy, scale=-1.0)
-        nc.scalar.activation(neg_unit[:], unit_sb[:], ACT.Copy, scale=-1.0)
-
         def pieces(n):
             return [slice(S // n * h, S // n * (h + 1)) for h in range(n)]
 
-        def sweeps(t, after, before):
-            vn = velocity(w1_q, t)
+        lam2 = [keep.tile([P, PACK, 2, P], F32, name="lam2_%d" % h) for h in range(2)]
+        fric = [keep.tile([P, PACK, 2, P], F32, name="fric_%d" % h) for h in range(2)]
+
+        def dealt(turned):
+            return turned.rearrange("p (b m t) -> p t b m", b=2, t=PACK)
+
+        def sweeps(c, parts):
+            vn = velocity("w1", c)
             na = work.tile([P, S], F32, name="na")
-            nc.vector.scalar_tensor_tensor(na[:], vn[:], -1.0, m_sb[t][:], ALU.mult, ALU.mult)
+            nc.vector.scalar_tensor_tensor(na[:], vn[:], -1.0, m_sb[c][:], ALU.mult, ALU.mult)
             m2 = work.tile([P, S], F32, name="m2")
-            nc.scalar.activation(m2[:], m_sb[t][:], ACT.Square)
+            nc.scalar.activation(m2[:], m_sb[c][:], ACT.Square)
             d = work.tile([P, S], F32, name="d")
             lam1 = work.tile([P, S], F32, name="lam1")
-            for cols in pieces(before):
-                nc.vector.tensor_tensor(d[:, cols], l_sb[t][:, cols], na[:, cols], ALU.add)
+            for cols in pieces(parts):
+                nc.vector.tensor_tensor(d[:, cols], l_sb[c][:, cols], na[:, cols], ALU.add)
                 nc.scalar.activation(lam1[:, cols], d[:, cols], ACT.Relu)
             lo = work.tile([P, S], F32, name="lo")
-            for h in range(2):
-                nc.scalar.activation(lo[:, HALF * h : HALF * (h + 1)], lam1[:].indirect(bod_sb[:, 16 * h : 16 * (h + 1)]), ACT.Copy)
+            for h, cols in enumerate(pieces(2)):
+                nc.scalar.activation(lo[:, cols], lam1[:].indirect(bod_sb[:, 16 * h : 16 * (h + 1)]), ACT.Copy)
             ng = work.tile([P, S], F32, name="ng")
-            lam2_t = work.tile([P, S], F32, name="lam2_t")
-            banks = []
-            for cols in pieces(after):
+            for cols in pieces(parts):
                 width = cols.stop - cols.start
                 nc.vector.scalar_tensor_tensor(ng[:, cols], lo[:, cols], -0.6, m2[:, cols], ALU.mult, ALU.mult)
-                f_t = psum.tile([P, width], F32, name="f_t", bufs=2)
+                f_t = bank("ft", width)
                 blocks = list(range(0, width, P))
                 for a, term in enumerate((na, lam1, ng)):
                     for b in blocks:
                         nc.tensor.matmul(f_t[:, b : b + P], term[:, cols.start + b : cols.start + b + P], ident[:], start=(a == 0 and b == 0), stop=(a == 2 and b == blocks[-1]), is_transpose=True)
-                nc.scalar.activation(lam2_t[:, cols], f_t[:], ACT.Relu)
-                bank = psum.tile([P, width], F32, name="lam2", bufs=3)
-                for b in blocks:
-                    nc.tensor.transpose(bank[:, b : b + P], lam2_t[:, cols.start + b : cols.start + b + P], ident[:])
-                banks.append((cols, bank))
-            return banks
+                for b in range(0, width, HALF):
+                    nc.scalar.activation(lam2[(cols.start + b) // HALF][:, :, :, 32 * c : 32 * (c + 1)], dealt(f_t[:, b : b + HALF]), ACT.Relu)
 
-        hid_rows = keep.tile([P, PACK, S], BF16, name="hid_rows")
+        def tangent(c):
+            vt = velocity("w2", c)
+            nb = work.tile([P, S], F32, name="nb")
+            nc.vector.scalar_tensor_tensor(nb[:], vt[:], -1.0, m_sb[c][:], ALU.mult, ALU.mult)
+            turned = bank("nbk", S)
+            for b in range(0, S, P):
+                nc.tensor.transpose(turned[:, b : b + P], nb[:, b : b + P], ident[:])
+            return turned
 
-        def tangent(t):
-            vt = velocity(w2_q, t)
-            nb_t = work.tile([P, S], F32, name="nb_t")
-            nc.vector.scalar_tensor_tensor(nb_t[:], vt[:], neg_unit[:, t : t + 1], m_sb[t][:], ALU.mult, ALU.mult)
-            return nb_t
+        def friction(c, turned):
+            own = slice(32 * c, 32 * (c + 1))
+            below = [work.tile([P, PACK, 2, 32], F32, name="below") for h in range(2)]
+            for h, cols in enumerate(pieces(2)):
+                nc.vector.scalar_tensor_tensor(below[h][:], lam2[h][:, :, :, own], 0.6, dealt(turned[:, cols]), ALU.mult, ALU.min)
+            for h in range(2):
+                nc.vector.scalar_tensor_tensor(fric[h][:, :, :, own], lam2[h][:, :, :, own], -0.6, below[h][:], ALU.mult, ALU.max)
 
-        def friction(t, banks, nb_t):
-            t1 = work.tile([P, S], F32, name="t1")
-            t2 = work.tile([P, S], F32, name="t2")
-            for cols, bank in banks:
-                nc.vector.scalar_tensor_tensor(t1[:, cols], bank[:], cone_hi[:, t : t + 1], nb_t[:, cols], ALU.mult, ALU.min)
-                nc.vector.scalar_tensor_tensor(t2[:, cols], bank[:], cone_lo[:, t : t + 1], t1[:, cols], ALU.mult, ALU.max)
-                nc.vector.scalar_tensor_tensor(hid_rows[:, t, cols], bank[:], unit_sb[:, t : t + 1], t2[:, cols], ALU.mult, ALU.add)
+        sweeps(0, 1)
+        wq["w2", 0] = weight_codes("w2", 0, (nc.vector.tensor_copy, nc.vector.tensor_copy))
+        sweeps(1, 1)
+        wq["w1", 1] = weight_codes("w1", 1, (nc.scalar.copy, nc.vector.tensor_copy))
+        nb_t[0] = tangent(0)
+        sweeps(2, 1)
+        friction(0, nb_t[0])
+        nb_t[1] = tangent(1)
+        wq["w2", 1] = weight_codes("w2", 1, (nc.scalar.copy, nc.scalar.copy))
+        sweeps(3, 2)
+        friction(1, nb_t[1])
+        nb_t[2] = tangent(2)
+        nb_t[3] = tangent(3)
+        friction(2, nb_t[2])
+        w3_q = quantize("w3", interleave("w3", w3_raw, nc.scalar.copy))
+        friction(3, nb_t[3])
 
-        w2_q = [quantize("w2q0", deal("w2g0", w2_raw[0], nc.vector.tensor_copy)[:], H)]
-        w2_q.append(quantize("w2q1", deal("w2g1", w2_raw[1], nc.vector.tensor_copy)[:], H))
-        lam2[0] = sweeps(0, 1, 1)
-        lam2[1] = sweeps(1, 1, 1)
-        lam2[2] = sweeps(2, 1, 1)
-        lam2[3] = sweeps(3, 2, 2)
-        nb[0] = tangent(0)
-        friction(0, lam2[0], nb[0])
-        nb[1] = tangent(1)
-        friction(1, lam2[1], nb[1])
-        nb[2] = tangent(2)
-        friction(2, lam2[2], nb[2])
-        nb[3] = tangent(3)
-        w3_bf = keep.tile([P, N * PACK], BF16, name="w3_bf", align_bytes=64)
-        nc.scalar.copy(out=w3_bf[:].rearrange("p (c i j) -> p c j i", i=4, j=PACK), in_=w3_raw[:].rearrange("p j (c i) -> p c j i", i=4))
-        w3_codes, w3_scales = quantize("w3q", w3_bf[:], N)
-        friction(3, lam2[3], nb[3])
-
-        for h, copy in enumerate((nc.scalar.copy, nc.vector.tensor_copy)):
-            cols = slice(HALF * h, HALF * (h + 1))
+        back_tags = ["mm","mm","ft","ft"]
+        for h, cols in enumerate(pieces(2)):
             hid = work.tile([P, HALF * PACK], BF16, name="hid", align_bytes=64)
-            copy(out=hid[:].rearrange("p (c i t) -> p c t i", i=4, t=PACK), in_=hid_rows[:, :, cols].rearrange("p t (c i) -> p c t i", i=4))
-            codes, scales = quantize("hid%d" % h, hid[:], HALF)
-            acc = psum.tile([P, HALF], F32, name="acc_out", tag="mm", bufs=3)
-            nc.tensor.matmul_mx(out=acc[:], lhsT=w3_codes[:].bitcast(FP8X4), lhsT_scale=w3_scales[:], rhs=codes[:].bitcast(FP8X4), rhs_scale=scales[:], start=True, stop=True)
+            for b in range(2):
+                total = bank(back_tags[2 * h + b], S)
+                for a, term in enumerate((lam2[h], fric[h])):
+                    for t in range(PACK):
+                        nc.tensor.matmul(total[:, P * t : P * (t + 1)], term[:, t, b, :], ident[:], start=(a == 0 and t == 0), stop=(a == 1 and t == PACK - 1), is_transpose=True)
+                nc.vector.tensor_tensor(
+                    hid[:, S * b : S * (b + 1)].rearrange("p (j t) -> p j t", t=PACK),
+                    total[:].rearrange("p (t j) -> p j t", t=PACK),
+                    unit_sb[:].unsqueeze(1).to_broadcast([P, P, PACK]),
+                    ALU.mult,
+                )
+            codes, scales = quantize("hid%d" % h, hid)
+            acc = bank("nbk", HALF)
+            nc.tensor.matmul_mx(out=acc[:], lhsT=w3_q[0][:].bitcast(FP8X4), lhsT_scale=w3_q[1][:], rhs=codes[:].bitcast(FP8X4), rhs_scale=scales[:], start=True, stop=True)
             res = work.tile([P, HALF], F32, name="res")
             nc.scalar.copy(out=res[:], in_=acc[:])
             nc.sync.dma_start(out=out[:, cols], in_=res[:])

@@ -53,8 +53,6 @@ def tile_picked_ycontc_sum_p_kernel(tc, x_words, x_scales, w1, w2, minv, lam0, u
 
         scale_tab = keep.tile([P, T], U8, name="scale_tab", align_bytes=64)
         nc.gpsimd.memset(scale_tab[:].bitcast(I32), 0)
-        ident = keep.tile([P, P], F32, name="ident")
-        make_identity(nc, ident[:])
 
         raw, wq, m_sb, l_sb, nb_t = {}, {}, {}, {}, {}
         offs_sb = keep.tile([P, S // 16], U16, name="offs_sb")
@@ -65,7 +63,9 @@ def tile_picked_ycontc_sum_p_kernel(tc, x_words, x_scales, w1, w2, minv, lam0, u
         nc.sync.dma_start(bod_sb[:], bod)
         raw["w1", 0] = load_weight(w1, "w1", 0)
         for q in range(4):
-            nc.sync.dma_start(out=scale_tab[32 * q : 32 * q + 4 * PASSES, :].bitcast(I32), in_=x_scales[:, 4 * q : 4 * q + 4, :].bitcast(I32))
+            nc.gpsimd.dma_start(out=scale_tab[32 * q : 32 * q + 4 * PASSES, :].bitcast(I32), in_=x_scales[:, 4 * q : 4 * q + 4, :].bitcast(I32))
+        ident = keep.tile([P, P], F32, name="ident")
+        make_identity(nc, ident[:])
         word_tab = [load_words(o) for o in range(PASSES)]
         m_sb[0] = load_rows(minv, "minv", 0)
         l_sb[0] = load_rows(lam0, "lam0", 0)
@@ -88,8 +88,8 @@ def tile_picked_ycontc_sum_p_kernel(tc, x_words, x_scales, w1, w2, minv, lam0, u
             nc.vector.quantize_mx(out=codes[:].bitcast(FP8X4), scales=scales[:], in_=grouped[:])
             return codes, scales
 
-        def interleave(name, rows, copy):
-            grouped = keep.tile([P, PACK * rows.shape[2]], BF16, name=name + "_bf", align_bytes=64)
+        def interleave(name, rows, copy, tag=None):
+            grouped = keep.tile([P, PACK * rows.shape[2]], BF16, name=name + "_bf", tag=tag or name, align_bytes=64)
             copy(out=grouped[:].rearrange("p (c i j) -> p c j i", i=4, j=PACK), in_=rows[:].rearrange("p j (c i) -> p c j i", i=4))
             return grouped
 
@@ -144,7 +144,7 @@ def tile_picked_ycontc_sum_p_kernel(tc, x_words, x_scales, w1, w2, minv, lam0, u
             lo = work.tile([P, S], F32, name="lo")
             for h, cols in enumerate(pieces(2)):
                 nc.scalar.activation(lo[:, cols], lam1[:].indirect(bod_sb[:, 16 * h : 16 * (h + 1)]), ACT.Copy)
-            ng = work.tile([P, S], F32, name="ng")
+            ng = keep.tile([P, S], F32, name="ng%d" % c, tag="ng%d" % c, align_bytes=64)
             for cols in pieces(parts):
                 width = cols.stop - cols.start
                 nc.vector.scalar_tensor_tensor(ng[:, cols], lo[:, cols], -0.6, m2[:, cols], ALU.mult, ALU.mult)
@@ -174,7 +174,7 @@ def tile_picked_ycontc_sum_p_kernel(tc, x_words, x_scales, w1, w2, minv, lam0, u
                 nc.vector.scalar_tensor_tensor(fric[h][:, :, :, own], lam2[h][:, :, :, own], -0.6, below[h][:], ALU.mult, ALU.max)
 
         sweeps(0, 1)
-        wq["w2", 0] = weight_codes("w2", 0, (nc.vector.tensor_copy, nc.vector.tensor_copy))
+        wq["w2", 0] = weight_codes("w2", 0, (nc.scalar.copy, nc.vector.tensor_copy))
         sweeps(1, 1)
         wq["w1", 1] = weight_codes("w1", 1, (nc.scalar.copy, nc.vector.tensor_copy))
         nb_t[0] = tangent(0)
@@ -187,26 +187,27 @@ def tile_picked_ycontc_sum_p_kernel(tc, x_words, x_scales, w1, w2, minv, lam0, u
         nb_t[2] = tangent(2)
         nb_t[3] = tangent(3)
         friction(2, nb_t[2])
-        w3_q = quantize("w3", interleave("w3", w3_raw, nc.scalar.copy))
+        w3_q = quantize("w3", interleave("w3", w3_raw, nc.scalar.copy, "ng3"))
         friction(3, nb_t[3])
 
         back_tags = ["mm","mm","ft","ft"]
-        for h, cols in enumerate(pieces(2)):
-            hid = work.tile([P, HALF * PACK], BF16, name="hid", align_bytes=64)
-            for b in range(2):
-                total = bank(back_tags[2 * h + b], S)
-                for a, term in enumerate((lam2[h], fric[h])):
+        for blocks in ((0, 1), (2,), (3,)):
+            width = P * len(blocks)
+            hid = work.tile([P, width * PACK], BF16, name="hid", align_bytes=64)
+            for n, jc in enumerate(blocks):
+                total = bank(back_tags[jc], S)
+                for a, term in enumerate((lam2[jc // 2], fric[jc // 2])):
                     for t in range(PACK):
-                        nc.tensor.matmul(total[:, P * t : P * (t + 1)], term[:, t, b, :], ident[:], start=(a == 0 and t == 0), stop=(a == 1 and t == PACK - 1), is_transpose=True)
+                        nc.tensor.matmul(total[:, P * t : P * (t + 1)], term[:, t, jc % 2, :], ident[:], start=(a == 0 and t == 0), stop=(a == 1 and t == PACK - 1), is_transpose=True)
                 nc.vector.tensor_tensor(
-                    hid[:, S * b : S * (b + 1)].rearrange("p (j t) -> p j t", t=PACK),
+                    hid[:, S * n : S * (n + 1)].rearrange("p (j t) -> p j t", t=PACK),
                     total[:].rearrange("p (t j) -> p j t", t=PACK),
                     unit_sb[:].unsqueeze(1).to_broadcast([P, P, PACK]),
                     ALU.mult,
                 )
-            codes, scales = quantize("hid%d" % h, hid)
-            acc = bank("nbk", HALF)
+            codes, scales = quantize("hid%d" % blocks[0], hid)
+            acc = bank("nbk", width)
             nc.tensor.matmul_mx(out=acc[:], lhsT=w3_q[0][:].bitcast(FP8X4), lhsT_scale=w3_q[1][:], rhs=codes[:].bitcast(FP8X4), rhs_scale=scales[:], start=True, stop=True)
-            res = work.tile([P, HALF], F32, name="res")
+            res = work.tile([P, width], F32, name="res")
             nc.scalar.copy(out=res[:], in_=acc[:])
-            nc.sync.dma_start(out=out[:, cols], in_=res[:])
+            nc.sync.dma_start(out=out[:, P * blocks[0] : P * blocks[0] + width], in_=res[:])

@@ -18,26 +18,38 @@ ACT = mybir.ActivationFunctionType
 
 P = 128
 PACK = 4
-PASSES = K // (P * PACK)
+K_PASS = P * PACK
+PASSES = K // K_PASS
+GROUPS = H // P
 HALF = S // 2
+W_HALF = H // 2
+RUN = P // PACK
+LINE = 4
+MU = 0.6
 
 
 def tile_picked_ycontc_sum_p_kernel(tc, x_words, x_scales, w1, w2, minv, lam0, unit, w3, offs, bod, out):
     nc = tc.nc
+    scalar_copy, vector_copy = nc.scalar.copy, nc.vector.tensor_copy
     with ExitStack() as ctx:
         keep = ctx.enter_context(tc.tile_pool(name="keep", bufs=1))
-        work = ctx.enter_context(tc.tile_pool(name="work", bufs=4))
+        work = ctx.enter_context(tc.tile_pool(name="work", bufs=GROUPS))
         psum = ctx.enter_context(tc.psum_pool(name="psum", bufs=1))
-        banks = {"mm": 3, "ft": 3, "nbk": 2, "bk": 1}
+
+        banks = {"product": 3, "sweep": 3, "tangent": 2}
 
         def bank(tag, width):
             return psum.tile([P, width], F32, name="bank_" + tag, tag=tag, bufs=banks[tag])
 
+        def pieces(n):
+            return [slice(S // n * h, S // n * (h + 1)) for h in range(n)]
+
         def load_weight(w, name, h):
             tiles = []
             for o in range(PASSES):
-                tile = keep.tile([P, PACK, H // 2], F32, name="%s_raw%d%d" % (name, h, o))
-                nc.sync.dma_start(out=tile[:], in_=w[512 * o : 512 * (o + 1), H // 2 * h : H // 2 * (h + 1)].rearrange("(p j) c -> p j c", j=PACK))
+                tile = keep.tile([P, PACK, W_HALF], F32, name="%s_raw%d%d" % (name, h, o))
+                rows = w[K_PASS * o : K_PASS * (o + 1), W_HALF * h : W_HALF * (h + 1)]
+                nc.sync.dma_start(out=tile[:], in_=rows.rearrange("(p j) c -> p j c", j=PACK))
                 tiles.append(tile)
             return tiles
 
@@ -47,39 +59,51 @@ def tile_picked_ycontc_sum_p_kernel(tc, x_words, x_scales, w1, w2, minv, lam0, u
             return rows
 
         def load_words(o):
-            tab = keep.tile([P, T], I32, name="word_tab%d" % o, align_bytes=64)
-            nc.sync.dma_start(out=tab[:], in_=x_words[o].rearrange("p n r -> p (n r)").bitcast(I32))
-            return tab
+            table = keep.tile([P, T], I32, name="word_table%d" % o, align_bytes=64)
+            nc.sync.dma_start(out=table[:], in_=x_words[o].rearrange("p n r -> p (n r)").bitcast(I32))
+            return table
 
-        scale_tab = keep.tile([P, T], U8, name="scale_tab", align_bytes=64)
-        nc.gpsimd.memset(scale_tab[:].bitcast(I32), 0)
+        scale_table = keep.tile([P, T], U8, name="scale_table", align_bytes=64)
+        nc.gpsimd.memset(scale_table[:].bitcast(I32), 0)
+        ident = keep.tile([P, P], F32, name="ident")
+        make_identity(nc, ident[:])
 
-        raw, wq, m_sb, l_sb, nb_t = {}, {}, {}, {}, {}
         offs_sb = keep.tile([P, S // 16], U16, name="offs_sb")
         nc.sync.dma_start(offs_sb[:], offs)
         unit_sb = keep.tile([P, PACK], F32, name="unit_sb")
         nc.sync.dma_start(out=unit_sb[:], in_=unit.rearrange("(p t) o -> p (t o)", t=PACK))
         bod_sb = keep.tile([P, S // 16], U16, name="bod_sb")
         nc.sync.dma_start(bod_sb[:], bod)
-        raw["w1", 0] = load_weight(w1, "w1", 0)
+        raw = {("w1", 0): load_weight(w1, "w1", 0)}
         for q in range(4):
-            nc.gpsimd.dma_start(out=scale_tab[32 * q : 32 * q + 4 * PASSES, :].bitcast(I32), in_=x_scales[:, 4 * q : 4 * q + 4, :].bitcast(I32))
-        ident = keep.tile([P, P], F32, name="ident")
-        make_identity(nc, ident[:])
-        word_tab = [load_words(o) for o in range(PASSES)]
-        m_sb[0] = load_rows(minv, "minv", 0)
-        l_sb[0] = load_rows(lam0, "lam0", 0)
-        raw["w2", 0] = load_weight(w2, "w2", 0)
-        m_sb[1] = load_rows(minv, "minv", 1)
-        l_sb[1] = load_rows(lam0, "lam0", 1)
-        raw["w1", 1] = load_weight(w1, "w1", 1)
-        m_sb[2] = load_rows(minv, "minv", 2)
-        l_sb[2] = load_rows(lam0, "lam0", 2)
-        raw["w2", 1] = load_weight(w2, "w2", 1)
-        m_sb[3] = load_rows(minv, "minv", 3)
-        l_sb[3] = load_rows(lam0, "lam0", 3)
+            nc.sync.dma_start(
+                out=scale_table[32 * q : 32 * q + 4 * PASSES, :].bitcast(I32),
+                in_=x_scales[:, 4 * q : 4 * q + 4, :].bitcast(I32),
+            )
+        word_table = [load_words(o) for o in range(PASSES)]
+
+        next_weight = [
+            (w2, "w2", 0, (scalar_copy, vector_copy)),
+            (w1, "w1", 1, (scalar_copy, vector_copy)),
+            (w2, "w2", 1, (scalar_copy, scalar_copy)),
+        ]
+        minv_sb, lam0_sb = [], []
+        for c in range(GROUPS):
+            minv_sb.append(load_rows(minv, "minv", c))
+            lam0_sb.append(load_rows(lam0, "lam0", c))
+            if c < len(next_weight):
+                w, name, h, copies = next_weight[c]
+                raw[name, h] = load_weight(w, name, h)
         w3_raw = keep.tile([P, PACK, N], F32, name="w3_raw")
         nc.sync.dma_start(out=w3_raw[:], in_=w3.rearrange("(p j) c -> p j c", j=PACK))
+
+        def interleave(name, rows, copy, tag):
+            grouped = keep.tile([P, PACK * rows.shape[2]], BF16, name=name + "_bf", tag=tag, align_bytes=64)
+            copy(
+                out=grouped[:].rearrange("p (c i j) -> p c j i", i=LINE, j=PACK),
+                in_=rows[:].rearrange("p j (c i) -> p c j i", i=LINE),
+            )
+            return grouped
 
         def quantize(name, grouped):
             width = grouped.shape[1] // PACK
@@ -88,28 +112,25 @@ def tile_picked_ycontc_sum_p_kernel(tc, x_words, x_scales, w1, w2, minv, lam0, u
             nc.vector.quantize_mx(out=codes[:].bitcast(FP8X4), scales=scales[:], in_=grouped[:])
             return codes, scales
 
-        def interleave(name, rows, copy, tag=None):
-            grouped = keep.tile([P, PACK * rows.shape[2]], BF16, name=name + "_bf", tag=tag or name, align_bytes=64)
-            copy(out=grouped[:].rearrange("p (c i j) -> p c j i", i=4, j=PACK), in_=rows[:].rearrange("p j (c i) -> p c j i", i=4))
-            return grouped
-
         def weight_codes(name, h, copies):
-            return [quantize("%s_%d%d" % (name, h, o), interleave("%s_%d%d" % (name, h, o), raw[name, h][o], copies[o])) for o in range(PASSES)]
+            labels = ["%s_%d%d" % (name, h, o) for o in range(PASSES)]
+            return [quantize(labels[o], interleave(labels[o], raw[name, h][o], copies[o], labels[o])) for o in range(PASSES)]
 
-        wq["w1", 0] = weight_codes("w1", 0, (nc.scalar.copy, nc.scalar.copy))
+        w_mx = {("w1", 0): weight_codes("w1", 0, (scalar_copy, scalar_copy))}
+
         x_scale = keep.tile([P, S], U8, name="x_scale", align_bytes=64)
-        nc.vector.tensor_copy(x_scale[:], scale_tab[:].indirect(offs_sb[:]))
+        nc.vector.tensor_copy(x_scale[:], scale_table[:].indirect(offs_sb[:]))
         x_code = []
         for o in range(PASSES):
             code = keep.tile([P, S], U32, name="x_code%d" % o, align_bytes=64)
-            nc.vector.tensor_copy(code[:], word_tab[o][:].bitcast(U32).indirect(offs_sb[:]))
+            nc.vector.tensor_copy(code[:], word_table[o][:].bitcast(U32).indirect(offs_sb[:]))
             x_code.append(code)
 
         def velocity(name, c):
-            acc = bank("mm", S)
+            acc = bank("product", S)
             cols = slice(P * (c % 2), P * (c % 2 + 1))
             for o in range(PASSES):
-                codes, scales = wq[name, c // 2][o]
+                codes, scales = w_mx[name, c // 2][o]
                 nc.tensor.matmul_mx(
                     out=acc[:],
                     lhsT=codes[:, cols].bitcast(FP8X4),
@@ -121,93 +142,112 @@ def tile_picked_ycontc_sum_p_kernel(tc, x_words, x_scales, w1, w2, minv, lam0, u
                 )
             return acc
 
-        def pieces(n):
-            return [slice(S // n * h, S // n * (h + 1)) for h in range(n)]
-
         lam2 = [keep.tile([P, PACK, 2, P], F32, name="lam2_%d" % h) for h in range(2)]
         fric = [keep.tile([P, PACK, 2, P], F32, name="fric_%d" % h) for h in range(2)]
 
         def dealt(turned):
             return turned.rearrange("p (b m t) -> p t b m", b=2, t=PACK)
 
-        def sweeps(c, parts):
+        def sweeps(c):
+            parts = pieces(2 if c == GROUPS - 1 else 1)
             vn = velocity("w1", c)
-            na = work.tile([P, S], F32, name="na")
-            nc.vector.scalar_tensor_tensor(na[:], vn[:], -1.0, m_sb[c][:], ALU.mult, ALU.mult)
-            m2 = work.tile([P, S], F32, name="m2")
-            nc.scalar.activation(m2[:], m_sb[c][:], ACT.Square)
-            d = work.tile([P, S], F32, name="d")
+            push = work.tile([P, S], F32, name="push")
+            nc.vector.scalar_tensor_tensor(push[:], vn[:], -1.0, minv_sb[c][:], ALU.mult, ALU.mult)
+            minv2 = work.tile([P, S], F32, name="minv2")
+            nc.scalar.activation(minv2[:], minv_sb[c][:], ACT.Square)
+            trial = work.tile([P, S], F32, name="trial")
             lam1 = work.tile([P, S], F32, name="lam1")
-            for cols in pieces(parts):
-                nc.vector.tensor_tensor(d[:, cols], l_sb[c][:, cols], na[:, cols], ALU.add)
-                nc.scalar.activation(lam1[:, cols], d[:, cols], ACT.Relu)
+            for cols in parts:
+                nc.vector.tensor_tensor(trial[:, cols], lam0_sb[c][:, cols], push[:, cols], ALU.add)
+                nc.scalar.activation(lam1[:, cols], trial[:, cols], ACT.Relu)
             lo = work.tile([P, S], F32, name="lo")
             for h, cols in enumerate(pieces(2)):
-                nc.scalar.activation(lo[:, cols], lam1[:].indirect(bod_sb[:, 16 * h : 16 * (h + 1)]), ACT.Copy)
-            ng = keep.tile([P, S], F32, name="ng%d" % c, tag="ng%d" % c, align_bytes=64)
-            for cols in pieces(parts):
+                entries = bod_sb[:, HALF // 16 * h : HALF // 16 * (h + 1)]
+                nc.scalar.activation(lo[:, cols], lam1[:].indirect(entries), ACT.Copy)
+            pull = keep.tile([P, S], F32, name="pull%d" % c, tag="pull%d" % c, align_bytes=64)
+            for cols in parts:
                 width = cols.stop - cols.start
-                nc.vector.scalar_tensor_tensor(ng[:, cols], lo[:, cols], -0.6, m2[:, cols], ALU.mult, ALU.mult)
-                f_t = bank("ft", width)
-                blocks = list(range(0, width, P))
-                for a, term in enumerate((na, lam1, ng)):
-                    for b in blocks:
-                        nc.tensor.matmul(f_t[:, b : b + P], term[:, cols.start + b : cols.start + b + P], ident[:], start=(a == 0 and b == 0), stop=(a == 2 and b == blocks[-1]), is_transpose=True)
-                for b in range(0, width, HALF):
-                    nc.scalar.activation(lam2[(cols.start + b) // HALF][:, :, :, 32 * c : 32 * (c + 1)], dealt(f_t[:, b : b + HALF]), ACT.Relu)
+                nc.vector.scalar_tensor_tensor(pull[:, cols], lo[:, cols], -MU, minv2[:, cols], ALU.mult, ALU.mult)
+                total = bank("sweep", width)
+                starts = list(range(0, width, P))
+                for a, term in enumerate((push, lam1, pull)):
+                    for s in starts:
+                        nc.tensor.matmul(
+                            total[:, s : s + P],
+                            term[:, cols.start + s : cols.start + s + P],
+                            ident[:],
+                            start=(a == 0 and s == 0),
+                            stop=(a == 2 and s == starts[-1]),
+                            is_transpose=True,
+                        )
+                for s in range(0, width, HALF):
+                    own = lam2[(cols.start + s) // HALF][:, :, :, RUN * c : RUN * (c + 1)]
+                    nc.scalar.activation(own, dealt(total[:, s : s + HALF]), ACT.Relu)
 
         def tangent(c):
             vt = velocity("w2", c)
-            nb = work.tile([P, S], F32, name="nb")
-            nc.vector.scalar_tensor_tensor(nb[:], vt[:], -1.0, m_sb[c][:], ALU.mult, ALU.mult)
-            turned = bank("nbk", S)
-            for b in range(0, S, P):
-                nc.tensor.transpose(turned[:, b : b + P], nb[:, b : b + P], ident[:])
+            slide = work.tile([P, S], F32, name="slide")
+            nc.vector.scalar_tensor_tensor(slide[:], vt[:], -1.0, minv_sb[c][:], ALU.mult, ALU.mult)
+            turned = bank("tangent", S)
+            for s in range(0, S, P):
+                nc.tensor.transpose(turned[:, s : s + P], slide[:, s : s + P], ident[:])
             return turned
 
         def friction(c, turned):
-            own = slice(32 * c, 32 * (c + 1))
-            below = [work.tile([P, PACK, 2, 32], F32, name="below") for h in range(2)]
+            own = slice(RUN * c, RUN * (c + 1))
+            below = [work.tile([P, PACK, 2, RUN], F32, name="below") for h in range(2)]
             for h, cols in enumerate(pieces(2)):
-                nc.vector.scalar_tensor_tensor(below[h][:], lam2[h][:, :, :, own], 0.6, dealt(turned[:, cols]), ALU.mult, ALU.min)
+                nc.vector.scalar_tensor_tensor(below[h][:], lam2[h][:, :, :, own], MU, dealt(turned[:, cols]), ALU.mult, ALU.min)
             for h in range(2):
-                nc.vector.scalar_tensor_tensor(fric[h][:, :, :, own], lam2[h][:, :, :, own], -0.6, below[h][:], ALU.mult, ALU.max)
+                nc.vector.scalar_tensor_tensor(fric[h][:, :, :, own], lam2[h][:, :, :, own], -MU, below[h][:], ALU.mult, ALU.max)
 
-        sweeps(0, 1)
-        wq["w2", 0] = weight_codes("w2", 0, (nc.scalar.copy, nc.vector.tensor_copy))
-        sweeps(1, 1)
-        wq["w1", 1] = weight_codes("w1", 1, (nc.scalar.copy, nc.vector.tensor_copy))
-        nb_t[0] = tangent(0)
-        sweeps(2, 1)
-        friction(0, nb_t[0])
-        nb_t[1] = tangent(1)
-        wq["w2", 1] = weight_codes("w2", 1, (nc.scalar.copy, nc.scalar.copy))
-        sweeps(3, 2)
-        friction(1, nb_t[1])
-        nb_t[2] = tangent(2)
-        nb_t[3] = tangent(3)
-        friction(2, nb_t[2])
-        w3_q = quantize("w3", interleave("w3", w3_raw, nc.scalar.copy, "ng3"))
-        friction(3, nb_t[3])
+        slides = {}
+        for c in range(GROUPS + 2):
+            if c < GROUPS:
+                sweeps(c)
+            if c >= 2:
+                friction(c - 2, slides[c - 2])
+            if 1 <= c <= GROUPS:
+                slides[c - 1] = tangent(c - 1)
+            if c < len(next_weight):
+                w, name, h, copies = next_weight[c]
+                w_mx[name, h] = weight_codes(name, h, copies)
+            if c == GROUPS:
+                w3_codes, w3_scales = quantize("w3", interleave("w3", w3_raw, scalar_copy, "pull%d" % (GROUPS - 1)))
 
-        back_tags = ["mm","mm","ft","ft"]
+        back_tags = ("product", "product", "sweep", "sweep")
         for blocks in ((0, 1), (2,), (3,)):
             width = P * len(blocks)
             hid = work.tile([P, width * PACK], BF16, name="hid", align_bytes=64)
-            for n, jc in enumerate(blocks):
-                total = bank(back_tags[jc], S)
-                for a, term in enumerate((lam2[jc // 2], fric[jc // 2])):
+            for n, jb in enumerate(blocks):
+                planes = bank(back_tags[jb], PACK * P)
+                for a, term in enumerate((lam2[jb // 2], fric[jb // 2])):
                     for t in range(PACK):
-                        nc.tensor.matmul(total[:, P * t : P * (t + 1)], term[:, t, jc % 2, :], ident[:], start=(a == 0 and t == 0), stop=(a == 1 and t == PACK - 1), is_transpose=True)
+                        nc.tensor.matmul(
+                            planes[:, P * t : P * (t + 1)],
+                            term[:, t, jb % 2, :],
+                            ident[:],
+                            start=(a == 0 and t == 0),
+                            stop=(a == 1 and t == PACK - 1),
+                            is_transpose=True,
+                        )
                 nc.vector.tensor_tensor(
-                    hid[:, S * n : S * (n + 1)].rearrange("p (j t) -> p j t", t=PACK),
-                    total[:].rearrange("p (t j) -> p j t", t=PACK),
+                    hid[:, PACK * P * n : PACK * P * (n + 1)].rearrange("p (j t) -> p j t", t=PACK),
+                    planes[:].rearrange("p (t j) -> p j t", t=PACK),
                     unit_sb[:].unsqueeze(1).to_broadcast([P, P, PACK]),
                     ALU.mult,
                 )
-            codes, scales = quantize("hid%d" % blocks[0], hid)
-            acc = bank("nbk", width)
-            nc.tensor.matmul_mx(out=acc[:], lhsT=w3_q[0][:].bitcast(FP8X4), lhsT_scale=w3_q[1][:], rhs=codes[:].bitcast(FP8X4), rhs_scale=scales[:], start=True, stop=True)
-            res = work.tile([P, width], F32, name="res")
-            nc.scalar.copy(out=res[:], in_=acc[:])
-            nc.sync.dma_start(out=out[:, P * blocks[0] : P * blocks[0] + width], in_=res[:])
+            hid_codes, hid_scales = quantize("hid%d" % blocks[0], hid)
+            acc = bank("tangent", width)
+            nc.tensor.matmul_mx(
+                out=acc[:],
+                lhsT=w3_codes[:].bitcast(FP8X4),
+                lhsT_scale=w3_scales[:],
+                rhs=hid_codes[:].bitcast(FP8X4),
+                rhs_scale=hid_scales[:],
+                start=True,
+                stop=True,
+            )
+            result = work.tile([P, width], F32, name="result")
+            nc.scalar.copy(out=result[:], in_=acc[:])
+            nc.sync.dma_start(out=out[:, P * blocks[0] : P * blocks[0] + width], in_=result[:])

from contextlib import ExitStack

import concourse.mybir as mybir
from concourse.masks import make_identity

K, T, S, N, H = 1024, 2048, 512, 128, 512
FLOPS = 2 * (2 * K * H * S + H * N * S)

F32 = mybir.dt.float32
BF16 = mybir.dt.bfloat16
I32 = mybir.dt.int32
U32 = mybir.dt.uint32
U16 = mybir.dt.uint16
U8 = mybir.dt.uint8
FP8X4 = mybir.dt.float8_e4m3fn_x4
ALU = mybir.AluOpType
ACT = mybir.ActivationFunctionType

P = 128
PACK = 4
K_PASS = P * PACK
PASSES = K // K_PASS
GROUPS = H // P
HALF = S // 2
W_HALF = H // 2
RUN = P // PACK
LINE = 4
MU = 0.6


def tile_picked_ycontc_sum_p_kernel(tc, x_words, x_scales, w1, w2, minv, lam0, unit, w3, offs, bod, out):
    nc = tc.nc
    scalar_copy, vector_copy = nc.scalar.copy, nc.vector.tensor_copy
    with ExitStack() as ctx:
        keep = ctx.enter_context(tc.tile_pool(name="keep", bufs=1))
        work = ctx.enter_context(tc.tile_pool(name="work", bufs=GROUPS))
        psum = ctx.enter_context(tc.psum_pool(name="psum", bufs=1))

        banks = {"product": 3, "sweep": 3, "tangent": 2}

        def bank(tag, width):
            return psum.tile([P, width], F32, name="bank_" + tag, tag=tag, bufs=banks[tag])

        def pieces(n):
            return [slice(S // n * h, S // n * (h + 1)) for h in range(n)]

        def load_weight(w, name, h):
            tiles = []
            for o in range(PASSES):
                tile = keep.tile([P, PACK, W_HALF], F32, name="%s_raw%d%d" % (name, h, o))
                rows = w[K_PASS * o : K_PASS * (o + 1), W_HALF * h : W_HALF * (h + 1)]
                nc.sync.dma_start(out=tile[:], in_=rows.rearrange("(p j) c -> p j c", j=PACK))
                tiles.append(tile)
            return tiles

        def load_rows(src, name, c):
            rows = keep.tile([P, S], F32, name="%s%d" % (name, c))
            nc.sync.dma_start(out=rows[:], in_=src[P * c : P * (c + 1), :])
            return rows

        def load_words(o):
            table = keep.tile([P, T], I32, name="word_table%d" % o, align_bytes=64)
            nc.sync.dma_start(out=table[:], in_=x_words[o].rearrange("p n r -> p (n r)").bitcast(I32))
            return table

        scale_table = keep.tile([P, T], U8, name="scale_table", align_bytes=64)
        nc.gpsimd.memset(scale_table[:].bitcast(I32), 0)
        ident = keep.tile([P, P], F32, name="ident")
        make_identity(nc, ident[:])

        offs_sb = keep.tile([P, S // 16], U16, name="offs_sb")
        nc.sync.dma_start(offs_sb[:], offs)
        unit_sb = keep.tile([P, PACK], F32, name="unit_sb")
        nc.sync.dma_start(out=unit_sb[:], in_=unit.rearrange("(p t) o -> p (t o)", t=PACK))
        bod_sb = keep.tile([P, S // 16], U16, name="bod_sb")
        nc.sync.dma_start(bod_sb[:], bod)
        raw = {("w1", 0): load_weight(w1, "w1", 0)}
        for q in range(4):
            nc.sync.dma_start(
                out=scale_table[32 * q : 32 * q + 4 * PASSES, :].bitcast(I32),
                in_=x_scales[:, 4 * q : 4 * q + 4, :].bitcast(I32),
            )
        word_table = [load_words(o) for o in range(PASSES)]

        next_weight = [
            (w2, "w2", 0, (scalar_copy, vector_copy)),
            (w1, "w1", 1, (scalar_copy, vector_copy)),
            (w2, "w2", 1, (scalar_copy, scalar_copy)),
        ]
        minv_sb, lam0_sb = [], []
        for c in range(GROUPS):
            minv_sb.append(load_rows(minv, "minv", c))
            lam0_sb.append(load_rows(lam0, "lam0", c))
            if c < len(next_weight):
                w, name, h, copies = next_weight[c]
                raw[name, h] = load_weight(w, name, h)
        w3_raw = keep.tile([P, PACK, N], F32, name="w3_raw")
        nc.sync.dma_start(out=w3_raw[:], in_=w3.rearrange("(p j) c -> p j c", j=PACK))

        def interleave(name, rows, copy, tag):
            grouped = keep.tile([P, PACK * rows.shape[2]], BF16, name=name + "_bf", tag=tag, align_bytes=64)
            copy(
                out=grouped[:].rearrange("p (c i j) -> p c j i", i=LINE, j=PACK),
                in_=rows[:].rearrange("p j (c i) -> p c j i", i=LINE),
            )
            return grouped

        def quantize(name, grouped):
            width = grouped.shape[1] // PACK
            codes = keep.tile([P, width], U32, name=name + "_codes", align_bytes=64)
            scales = keep.tile([P, width], U8, name=name + "_scales", align_bytes=64)
            nc.vector.quantize_mx(out=codes[:].bitcast(FP8X4), scales=scales[:], in_=grouped[:])
            return codes, scales

        def weight_codes(name, h, copies):
            labels = ["%s_%d%d" % (name, h, o) for o in range(PASSES)]
            return [quantize(labels[o], interleave(labels[o], raw[name, h][o], copies[o], labels[o])) for o in range(PASSES)]

        w_mx = {("w1", 0): weight_codes("w1", 0, (scalar_copy, scalar_copy))}

        x_scale = keep.tile([P, S], U8, name="x_scale", align_bytes=64)
        nc.vector.tensor_copy(x_scale[:], scale_table[:].indirect(offs_sb[:]))
        x_code = []
        for o in range(PASSES):
            code = keep.tile([P, S], U32, name="x_code%d" % o, align_bytes=64)
            nc.vector.tensor_copy(code[:], word_table[o][:].bitcast(U32).indirect(offs_sb[:]))
            x_code.append(code)

        def velocity(name, c):
            acc = bank("product", S)
            cols = slice(P * (c % 2), P * (c % 2 + 1))
            for o in range(PASSES):
                codes, scales = w_mx[name, c // 2][o]
                nc.tensor.matmul_mx(
                    out=acc[:],
                    lhsT=codes[:, cols].bitcast(FP8X4),
                    lhsT_scale=scales[:, cols],
                    rhs=x_code[o][:].bitcast(FP8X4),
                    rhs_scale=x_scale[4 * o : P, :],
                    start=(o == 0),
                    stop=(o == PASSES - 1),
                )
            return acc

        lam2 = [keep.tile([P, PACK, 2, P], F32, name="lam2_%d" % h) for h in range(2)]
        fric = [keep.tile([P, PACK, 2, P], F32, name="fric_%d" % h) for h in range(2)]

        def dealt(turned):
            return turned.rearrange("p (b m t) -> p t b m", b=2, t=PACK)

        def sweeps(c):
            parts = pieces(2 if c == GROUPS - 1 else 1)
            vn = velocity("w1", c)
            push = work.tile([P, S], F32, name="push")
            nc.vector.scalar_tensor_tensor(push[:], vn[:], -1.0, minv_sb[c][:], ALU.mult, ALU.mult)
            minv2 = work.tile([P, S], F32, name="minv2")
            nc.scalar.activation(minv2[:], minv_sb[c][:], ACT.Square)
            trial = work.tile([P, S], F32, name="trial")
            lam1 = work.tile([P, S], F32, name="lam1")
            for cols in parts:
                nc.vector.tensor_tensor(trial[:, cols], lam0_sb[c][:, cols], push[:, cols], ALU.add)
                nc.scalar.activation(lam1[:, cols], trial[:, cols], ACT.Relu)
            lo = work.tile([P, S], F32, name="lo")
            for h, cols in enumerate(pieces(2)):
                entries = bod_sb[:, HALF // 16 * h : HALF // 16 * (h + 1)]
                nc.scalar.activation(lo[:, cols], lam1[:].indirect(entries), ACT.Copy)
            pull = keep.tile([P, S], F32, name="pull%d" % c, tag="pull%d" % c, align_bytes=64)
            for cols in parts:
                width = cols.stop - cols.start
                nc.vector.scalar_tensor_tensor(pull[:, cols], lo[:, cols], -MU, minv2[:, cols], ALU.mult, ALU.mult)
                total = bank("sweep", width)
                starts = list(range(0, width, P))
                for a, term in enumerate((push, lam1, pull)):
                    for s in starts:
                        nc.tensor.matmul(
                            total[:, s : s + P],
                            term[:, cols.start + s : cols.start + s + P],
                            ident[:],
                            start=(a == 0 and s == 0),
                            stop=(a == 2 and s == starts[-1]),
                            is_transpose=True,
                        )
                for s in range(0, width, HALF):
                    own = lam2[(cols.start + s) // HALF][:, :, :, RUN * c : RUN * (c + 1)]
                    nc.scalar.activation(own, dealt(total[:, s : s + HALF]), ACT.Relu)

        def tangent(c):
            vt = velocity("w2", c)
            slide = work.tile([P, S], F32, name="slide")
            nc.vector.scalar_tensor_tensor(slide[:], vt[:], -1.0, minv_sb[c][:], ALU.mult, ALU.mult)
            turned = bank("tangent", S)
            for s in range(0, S, P):
                nc.tensor.transpose(turned[:, s : s + P], slide[:, s : s + P], ident[:])
            return turned

        def friction(c, turned):
            own = slice(RUN * c, RUN * (c + 1))
            below = [work.tile([P, PACK, 2, RUN], F32, name="below") for h in range(2)]
            for h, cols in enumerate(pieces(2)):
                nc.vector.scalar_tensor_tensor(below[h][:], lam2[h][:, :, :, own], MU, dealt(turned[:, cols]), ALU.mult, ALU.min)
            for h in range(2):
                nc.vector.scalar_tensor_tensor(fric[h][:, :, :, own], lam2[h][:, :, :, own], -MU, below[h][:], ALU.mult, ALU.max)

        slides = {}
        for c in range(GROUPS + 2):
            if c < GROUPS:
                sweeps(c)
            if c >= 2:
                friction(c - 2, slides[c - 2])
            if 1 <= c <= GROUPS:
                slides[c - 1] = tangent(c - 1)
            if c < len(next_weight):
                w, name, h, copies = next_weight[c]
                w_mx[name, h] = weight_codes(name, h, copies)
            if c == GROUPS:
                w3_codes, w3_scales = quantize("w3", interleave("w3", w3_raw, scalar_copy, "pull%d" % (GROUPS - 1)))

        back_tags = ("product", "product", "sweep", "sweep")
        for blocks in ((0, 1), (2,), (3,)):
            width = P * len(blocks)
            hid = work.tile([P, width * PACK], BF16, name="hid", align_bytes=64)
            for n, jb in enumerate(blocks):
                planes = bank(back_tags[jb], PACK * P)
                for a, term in enumerate((lam2[jb // 2], fric[jb // 2])):
                    for t in range(PACK):
                        nc.tensor.matmul(
                            planes[:, P * t : P * (t + 1)],
                            term[:, t, jb % 2, :],
                            ident[:],
                            start=(a == 0 and t == 0),
                            stop=(a == 1 and t == PACK - 1),
                            is_transpose=True,
                        )
                nc.vector.tensor_tensor(
                    hid[:, PACK * P * n : PACK * P * (n + 1)].rearrange("p (j t) -> p j t", t=PACK),
                    planes[:].rearrange("p (t j) -> p j t", t=PACK),
                    unit_sb[:].unsqueeze(1).to_broadcast([P, P, PACK]),
                    ALU.mult,
                )
            hid_codes, hid_scales = quantize("hid%d" % blocks[0], hid)
            acc = bank("tangent", width)
            nc.tensor.matmul_mx(
                out=acc[:],
                lhsT=w3_codes[:].bitcast(FP8X4),
                lhsT_scale=w3_scales[:],
                rhs=hid_codes[:].bitcast(FP8X4),
                rhs_scale=hid_scales[:],
                start=True,
                stop=True,
            )
            result = work.tile([P, width], F32, name="result")
            nc.scalar.copy(out=result[:], in_=acc[:])
            nc.sync.dma_start(out=out[:, P * blocks[0] : P * blocks[0] + width], in_=result[:])
